import numpy as np
CORES = [6,14,22,30,38,46,54,62,134,142,150,158,166,174,182,190,262,270,278,286,294,302,310,318,390,398,406,414,422,430,438,446]
N = 32
GROUPS = [[0,1,2,3,4,5,6,7],[8,9,10,11,12,13,14,15],[16,17,18,19,20,21,22,23],[24,25,26,27,28,29,30,31]]
def setup_inputs(rng):
    return {"x": rng.standard_normal((N, 128, 1024), dtype=np.float32)}
def reference(x):
    y = np.empty((N, 128, 1024), x.dtype)
    for g in GROUPS:
        s = x[g].sum(axis=0, dtype=np.float64).astype(x[g].dtype)
        for r in g:
            y[r] = s
    return {"y": y}

@@ -1,0 +1,59 @@
+from concourse.bass import DstId, RemoteDMATransfer
+
+SCRATCH = {
+    "xd": ("dram", [8, 128, 128], "float32"),
+    "land": ("dram", [4, 128, 128], "float32"),
+    "res": ("dram", [8, 128, 128], "float32"),
+}
+SEMAPHORES = ["ld_a", "ld_b", "mate", "part", "own", "other", "sent", "st"]
+
+PAIR = [0x03, 0x0C, 0x30, 0xC0]
+
+
+def rank_program(g, core, T, topo):
+    S = T.sem
+
+    def did(dst):
+        rid, pid = topo.addr(dst, core)
+        return DstId(rid=rid, pnc=pid)
+
+    base = core - core % 128
+    chip = topo.chip(core)
+    p, k = chip % 2, chip // 2
+
+    def at(c, n):
+        return base + 8 * c + n
+
+    if T.rank_of(core) is not None:
+        o = 1 - p
+        mate = at(chip ^ 1, 6)
+        g.sync.dma_start(T.xd[4 * o:4 * o + 4], T.x[64 * o:64 * o + 64, :]).then_inc(S.ld_a, 16)
+        g.scalar.dma_start(T.xd[4 * p:4 * p + 4], T.x[64 * p:64 * p + 64, :]).then_inc(S.ld_b, 16)
+        g.wait_ge(S.ld_a, 16)
+        g.remote_dma_fused([
+            RemoteDMATransfer(dst_ids=[did(mate)], dma_engine_mask=PAIR[q], remote_sem=S.mate,
+                              src=T.xd[4 * o + q], dst=T.land[q]) for q in range(4)], local_sem=S.sent)
+        g.wait_ge(S.ld_b, 16)
+        g.wait_ge(S.mate, 8)
+        g.remote_dma_fused([
+            RemoteDMATransfer(dst_ids=[did(at(2 * q + p, 7))], dma_engine_mask=PAIR[q], remote_sem=S.part,
+                              srcs=[T.xd[4 * p + q], T.land[q]], dsts=[T.land[k]], alu_op=1) for q in range(4)],
+            local_sem=S.sent)
+        g.wait_ge(S.own, 32)
+        g.remote_dma_fused([
+            RemoteDMATransfer(dst_ids=[did(mate)], dma_engine_mask=PAIR[q], remote_sem=S.other,
+                              src=T.res[4 * p + q], dst=T.res[4 * p + q]) for q in range(4)], local_sem=S.sent)
+        g.sync.wait_ge(S.own, 32)
+        g.sync.dma_start(T.y[64 * p:64 * p + 64, :], T.res[4 * p:4 * p + 4]).then_inc(S.st, 16)
+        g.scalar.wait_ge(S.other, 8)
+        g.scalar.dma_start(T.y[64 * o:64 * o + 64, :], T.res[4 * o:4 * o + 4]).then_inc(S.st, 16)
+        g.wait_ge(S.other, 8)
+        g.wait_ge(S.sent, 24)
+        g.wait_ge(S.st, 32)
+    elif core % 8 == 7 and T.rank_of(core - 1) is not None:
+        g.wait_ge(S.part, 8)
+        g.remote_dma_fused([
+            RemoteDMATransfer(dst_ids=[did(at(2 * q + p, 6)) for q in range(4)], dma_engine_mask=0xFF,
+                              remote_sem=S.own, srcs=[T.land[q] for q in range(4)],
+                              dsts=[T.res[4 * p + k] for q in range(4)], alu_op=1)], local_sem=S.sent)
+        g.wait_ge(S.sent, 8)

@@ -1,59 +1,55 @@
 from concourse.bass import DstId, RemoteDMATransfer
 
 SCRATCH = {
-    "xd": ("dram", [8, 128, 128], "float32"),
-    "land": ("dram", [4, 128, 128], "float32"),
-    "res": ("dram", [8, 128, 128], "float32"),
+    "buf": ("dram", [16, 128, 64], "float32"),
 }
-SEMAPHORES = ["ld_a", "ld_b", "mate", "part", "own", "other", "sent", "st"]
+SEMAPHORES = ["ld0", "ld1", "part", "fin0", "fin1", "sent", "st"]
 
-PAIR = [0x03, 0x0C, 0x30, 0xC0]
+HELPER = (2, 3)
 
 
 def rank_program(g, core, T, topo):
     S = T.sem
+    first = core - core % 8
+
+    members, me = None, None
+    for grp in T.tables["GROUPS"]:
+        cs = [T.cores[r] for r in grp]
+        for i, c in enumerate(cs):
+            if c - c % 8 == first:
+                members, me = cs, i
+    if members is None:
+        return
+    n = len(members)
 
     def did(dst):
         rid, pid = topo.addr(dst, core)
         return DstId(rid=rid, pnc=pid)
 
-    base = core - core % 128
-    chip = topo.chip(core)
-    p, k = chip % 2, chip // 2
-
-    def at(c, n):
-        return base + 8 * c + n
-
-    if T.rank_of(core) is not None:
-        o = 1 - p
-        mate = at(chip ^ 1, 6)
-        g.sync.dma_start(T.xd[4 * o:4 * o + 4], T.x[64 * o:64 * o + 64, :]).then_inc(S.ld_a, 16)
-        g.scalar.dma_start(T.xd[4 * p:4 * p + 4], T.x[64 * p:64 * p + 64, :]).then_inc(S.ld_b, 16)
-        g.wait_ge(S.ld_a, 16)
-        g.remote_dma_fused([
-            RemoteDMATransfer(dst_ids=[did(mate)], dma_engine_mask=PAIR[q], remote_sem=S.mate,
-                              src=T.xd[4 * o + q], dst=T.land[q]) for q in range(4)], local_sem=S.sent)
-        g.wait_ge(S.ld_b, 16)
-        g.wait_ge(S.mate, 8)
-        g.remote_dma_fused([
-            RemoteDMATransfer(dst_ids=[did(at(2 * q + p, 7))], dma_engine_mask=PAIR[q], remote_sem=S.part,
-                              srcs=[T.xd[4 * p + q], T.land[q]], dsts=[T.land[k]], alu_op=1) for q in range(4)],
-            local_sem=S.sent)
-        g.wait_ge(S.own, 32)
-        g.remote_dma_fused([
-            RemoteDMATransfer(dst_ids=[did(mate)], dma_engine_mask=PAIR[q], remote_sem=S.other,
-                              src=T.res[4 * p + q], dst=T.res[4 * p + q]) for q in range(4)], local_sem=S.sent)
-        g.sync.wait_ge(S.own, 32)
-        g.sync.dma_start(T.y[64 * p:64 * p + 64, :], T.res[4 * p:4 * p + 4]).then_inc(S.st, 16)
-        g.scalar.wait_ge(S.other, 8)
-        g.scalar.dma_start(T.y[64 * o:64 * o + 64, :], T.res[4 * o:4 * o + 4]).then_inc(S.st, 16)
-        g.wait_ge(S.other, 8)
-        g.wait_ge(S.sent, 24)
+    if core == members[me]:
+        q = (g.sync, g.scalar)
+        ld = (S.ld0, S.ld1)
+        fin = (S.fin0, S.fin1)
+        for t in range(2):
+            q[t].dma_start(T.buf[n * t:n * t + n], T.x[64 * t:64 * t + 64, :]).then_inc(ld[t], 16)
+        for t in range(2):
+            g.wait_ge(ld[t], 16)
+            g.remote_dma_fused([
+                RemoteDMATransfer(dst_ids=[did(members[j] - members[j] % 8 + HELPER[t])], dma_engine_mask=1 << j,
+                                  remote_sem=S.part, src=T.buf[n * t + j], dst=T.buf[me]) for j in range(n)],
+                local_sem=S.sent)
+        for t in range(2):
+            q[t].wait_ge(fin[t], 8 * n)
+            q[t].dma_start(T.y[64 * t:64 * t + 64, :], T.buf[n * t:n * t + n]).then_inc(S.st, 16)
+        g.wait_ge(S.sent, 2 * n)
+        g.wait_ge(S.fin0, 8 * n)
+        g.wait_ge(S.fin1, 8 * n)
         g.wait_ge(S.st, 32)
-    elif core % 8 == 7 and T.rank_of(core - 1) is not None:
-        g.wait_ge(S.part, 8)
+    elif core % 8 in HELPER:
+        t = HELPER.index(core % 8)
+        g.wait_ge(S.part, n)
         g.remote_dma_fused([
-            RemoteDMATransfer(dst_ids=[did(at(2 * q + p, 6)) for q in range(4)], dma_engine_mask=0xFF,
-                              remote_sem=S.own, srcs=[T.land[q] for q in range(4)],
-                              dsts=[T.res[4 * p + k] for q in range(4)], alu_op=1)], local_sem=S.sent)
+            RemoteDMATransfer(dst_ids=[did(c) for c in members], dma_engine_mask=0xFF,
+                              remote_sem=(S.fin0, S.fin1)[t], srcs=[T.buf[i] for i in range(n)],
+                              dsts=[T.buf[n * t + me] for c in members], alu_op=1)], local_sem=S.sent)
         g.wait_ge(S.sent, 8)

from concourse.bass import DstId, RemoteDMATransfer

SCRATCH = {
    "buf": ("dram", [16, 128, 64], "float32"),
}
SEMAPHORES = ["ld0", "ld1", "part", "fin0", "fin1", "sent", "st"]

HELPER = (2, 3)


def rank_program(g, core, T, topo):
    S = T.sem
    first = core - core % 8

    members, me = None, None
    for grp in T.tables["GROUPS"]:
        cs = [T.cores[r] for r in grp]
        for i, c in enumerate(cs):
            if c - c % 8 == first:
                members, me = cs, i
    if members is None:
        return
    n = len(members)

    def did(dst):
        rid, pid = topo.addr(dst, core)
        return DstId(rid=rid, pnc=pid)

    if core == members[me]:
        q = (g.sync, g.scalar)
        ld = (S.ld0, S.ld1)
        fin = (S.fin0, S.fin1)
        for t in range(2):
            q[t].dma_start(T.buf[n * t:n * t + n], T.x[64 * t:64 * t + 64, :]).then_inc(ld[t], 16)
        for t in range(2):
            g.wait_ge(ld[t], 16)
            g.remote_dma_fused([
                RemoteDMATransfer(dst_ids=[did(members[j] - members[j] % 8 + HELPER[t])], dma_engine_mask=1 << j,
                                  remote_sem=S.part, src=T.buf[n * t + j], dst=T.buf[me]) for j in range(n)],
                local_sem=S.sent)
        for t in range(2):
            q[t].wait_ge(fin[t], 8 * n)
            q[t].dma_start(T.y[64 * t:64 * t + 64, :], T.buf[n * t:n * t + n]).then_inc(S.st, 16)
        g.wait_ge(S.sent, 2 * n)
        g.wait_ge(S.fin0, 8 * n)
        g.wait_ge(S.fin1, 8 * n)
        g.wait_ge(S.st, 32)
    elif core % 8 in HELPER:
        t = HELPER.index(core % 8)
        g.wait_ge(S.part, n)
        g.remote_dma_fused([
            RemoteDMATransfer(dst_ids=[did(c) for c in members], dma_engine_mask=0xFF,
                              remote_sem=(S.fin0, S.fin1)[t], srcs=[T.buf[i] for i in range(n)],
                              dsts=[T.buf[n * t + me] for c in members], alu_op=1)], local_sem=S.sent)
        g.wait_ge(S.sent, 8)
